import numpy as np
import ml_dtypes


def mxq(x, axis, fmt="e4m3"):
    dtype, down = {"e4m3": (ml_dtypes.float8_e4m3fn, 7), "e5m2": (ml_dtypes.float8_e5m2, 14)}[fmt]
    v = np.moveaxis(np.asarray(x, np.float32).astype(ml_dtypes.bfloat16).astype(np.float64), axis, -1)
    blocks = v.reshape(v.shape[:-1] + (-1, 32))
    amax = np.abs(blocks).max(-1, keepdims=True)
    byte = np.maximum(np.where(amax > 0, np.frexp(amax)[1] - 1 + 127, 0) - down, 1)
    scale = np.exp2(byte - 127.0)
    codes = (blocks / scale).astype(np.float32).astype(dtype).astype(np.float64)
    return np.moveaxis((codes * scale).reshape(v.shape), -1, axis)


WIDE = False


def mx_kscale(k):
    if not WIDE:
        return np.ones(k)
    levels = np.array([30, -30])
    if k % 512:
        return np.exp2(np.random.permutation(np.resize(levels, k // 32))).repeat(32)
    a = np.empty((k // 512, 16))
    for p in range(k // 512):
        a[p, :8] = np.random.permutation(np.resize(levels, 8))
        for g in range(8):
            far = levels[np.abs(levels - a[p, g]) >= 10]
            a[p, g + 8] = far[np.random.randint(len(far))]
    return np.exp2(a.ravel()).repeat(32)


def f64(x):
    return np.asarray(x).astype(np.float64)


def striped(idx):
    return np.tile(np.asarray(idx).reshape(-1, 16).T, (8, 1)).astype(np.uint16)


def unstriped(offs):
    return offs[:16].T.reshape(-1).astype(np.int64)


E2M1 = np.array([0.0, 0.5, 1.0, 1.5, 2.0, 3.0, 4.0, 6.0, -0.0, -0.5, -1.0, -1.5, -2.0, -3.0, -4.0, -6.0])


def pack_weight(w, fmt):
    k, n = w.shape
    w = f64(np.asarray(w, np.float32).astype(ml_dtypes.bfloat16)).reshape(k // 32, 32, n)
    amax = np.abs(w).max(1)
    if fmt in ("e4m3", "e5m2"):
        byte = np.frexp(amax)[1] - 1 + 127 - (7 if fmt == "e4m3" else 14)
    else:
        mant, ex = np.frexp(amax / 6.0)
        byte = np.where(mant > 0.5, ex, ex - 1) + 127
    byte = np.clip(np.where(amax > 0, byte, 1), 1, 254)
    scaled = (w * np.exp2(127.0 - byte)[:, None, :]).reshape(k, n).astype(np.float32)
    by_word = np.ascontiguousarray(scaled.reshape(k // 512, 128, 4, n).transpose(0, 1, 3, 2))
    if fmt in ("e4m3", "e5m2"):
        words = by_word.astype(ml_dtypes.float8_e4m3fn if fmt == "e4m3" else ml_dtypes.float8_e5m2).view(np.uint8)
    else:
        c = by_word.astype(ml_dtypes.float4_e2m1fn).view(np.uint8) & 0xF
        words = (c[..., 0::2] | (c[..., 1::2] << 4)).reshape(k // 512, 128, 2 * n)
    return np.ascontiguousarray(words), np.ascontiguousarray(byte.astype(np.uint8).reshape(k // 512, 16, n))


def unpack_weight(words, scales, fmt):
    g, _, n = scales.shape
    words = np.ascontiguousarray(words).reshape(g, 128, n, -1)
    if fmt in ("e4m3", "e5m2"):
        vals = words.view(ml_dtypes.float8_e4m3fn if fmt == "e4m3" else ml_dtypes.float8_e5m2).astype(np.float64)
    else:
        nib = np.empty((g, 128, n, 4), np.uint8)
        nib[..., 0::2] = words & 0xF
        nib[..., 1::2] = words >> 4
        vals = E2M1[nib]
    vals = vals * np.repeat(np.exp2(scales.astype(np.float64) - 127.0), 8, axis=1)[..., None]
    return vals.transpose(0, 1, 3, 2).reshape(g * 512, n)


def e4m3fn_bytes(y):
    return np.clip(np.asarray(y, np.float64), -448.0, 448.0).astype(np.float32).astype(ml_dtypes.float8_e4m3fn).view(np.uint8)


def e4m3fn_values(b):
    return np.asarray(b, np.uint8).view(ml_dtypes.float8_e4m3fn).astype(np.float64)


K, T, J, R, V, D, N = 512, 1024, 256, 512, 1024, 1024, 256


def setup_inputs():
    n = np.random.standard_normal
    idx = np.random.permutation(T)[:J]
    idx2 = np.random.permutation(V)[:J]
    idx3 = np.random.permutation(D)[:J]
    fk = mx_kscale(K)
    fr = mx_kscale(R)
    xtp = pack_weight(n((K, T)) / fk[:, None], "e4m3")
    wp = pack_weight(n((K, R)) * 1 / np.sqrt(K) * fk[:, None], "e2m1")
    w2p = pack_weight(n((K, R)) * 1 / np.sqrt(K) * fk[:, None], "e5m2")
    wbp = pack_weight(n((R, N)) * 1 / np.sqrt(R) / fr[:, None], "e5m2")
    return {
        "xt_words": xtp[0],
        "xt_scales": xtp[1],
        "w_words": wp[0],
        "w_scales": wp[1],
        "w2_words": w2p[0],
        "w2_scales": w2p[1],
        "ca": e4m3fn_bytes(60.0 * n((R, V))),
        "cb": e4m3fn_bytes(60.0 * n((R, D))),
        "sa": (np.random.uniform(0.004, 0.012, (R, 1)) * fr[:, None]).astype(np.float32),
        "sb": (np.random.uniform(0.004, 0.012, (R, 1)) * fr[:, None]).astype(np.float32),
        "wb_words": wbp[0],
        "wb_scales": wbp[1],
        "offs": striped(idx),
        "offs2": striped(idx2),
        "offs3": striped(idx3),
    }


def reference(xt_words, xt_scales, w_words, w_scales, w2_words, w2_scales, ca, cb, sa, sb, wb_words, wb_scales, offs, offs2, offs3):
    idx = unstriped(offs)
    idx2 = unstriped(offs2)
    idx3 = unstriped(offs3)
    xtu = unpack_weight(xt_words, xt_scales, "e4m3")
    wu = unpack_weight(w_words, w_scales, "e2m1")
    w2u = unpack_weight(w2_words, w2_scales, "e5m2")
    wbu = unpack_weight(wb_words, wb_scales, "e5m2")
    xtidxg = xtu[:, idx]
    a = wu.T @ xtidxg
    b = w2u.T @ xtidxg
    ga = e4m3fn_values(ca)[:, idx2] * f64(sa)
    gb = e4m3fn_values(cb)[:, idx3] * f64(sb)
    hid = np.maximum(a * ga, b * gb)
    hidq = mxq(hid, 0, "e4m3")
    p = wbu.T @ hidq
    return p

@@ -1,0 +1,193 @@
+from contextlib import ExitStack
+
+import concourse.mybir as mybir
+
+K, T, J, R, V, N = 512, 1024, 256, 512, 1024, 256
+FLOPS = 2 * (2 * K * R * J + R * N * J)
+
+F32 = mybir.dt.float32
+BF16 = mybir.dt.bfloat16
+I32 = mybir.dt.int32
+U32 = mybir.dt.uint32
+U16 = mybir.dt.uint16
+U8 = mybir.dt.uint8
+FP8 = mybir.dt.float8_e4m3fn
+E4M3X4 = mybir.dt.float8_e4m3fn_x4
+E5M2X4 = mybir.dt.float8_e5m2_x4
+E2M1X4 = mybir.dt.float4_e2m1fn_x4
+ALU = mybir.AluOpType
+ACT = mybir.ActivationFunctionType
+
+P = 128
+PACK = 4
+QUADS = 4
+HALF = J // 2
+RUN = 4
+
+
+def load_scale_rows(queue, plane, scales, q):
+    queue.dma_start(plane[32 * q : 32 * q + 4, :].bitcast(I32), scales[0, 4 * q : 4 * q + 4, :].bitcast(I32))
+
+
+def tile_list_twostores_kernel(
+    tc, xt_words, xt_scales, w_words, w_scales, w2_words, w2_scales, ca, cb, sa, sb, wb_words, wb_scales, offs, offs2, offs3, out
+):
+    nc = tc.nc
+    with ExitStack() as ctx:
+        sb_pool = ctx.enter_context(tc.tile_pool(name="keep", bufs=1))
+        psum = ctx.enter_context(tc.psum_pool(name="psum", bufs=1))
+
+        def tile(shape, dtype, name):
+            return sb_pool.tile(shape, dtype, name=name, align_bytes=64)
+
+        list_x = tile([P, J // 16], U16, "list_x")
+        list_a = tile([P, J // 16], U16, "list_a")
+        list_b = tile([P, J // 16], U16, "list_b")
+        x_words = tile([P, T], I32, "x_words")
+        x_plane = tile([P, T], U8, "x_plane")
+        w_raw = tile([P, 2 * R], U8, "w_raw")
+        w2_raw = tile([P, R], I32, "w2_raw")
+        w_plane_raw = tile([P, R], U8, "w_plane_raw")
+        w2_plane_raw = tile([P, R], U8, "w2_plane_raw")
+        wb_codes = tile([P, N], I32, "wb_codes")
+        wb_plane = tile([P, N], U8, "wb_plane")
+        step_a = tile([P, PACK], F32, "step_a")
+        step_b = tile([P, PACK], F32, "step_b")
+        store_a = [tile([P, V], U8, "store_a%d" % t) for t in range(PACK)]
+        store_b = [tile([P, V], U8, "store_b%d" % t) for t in range(PACK)]
+
+        nc.vector.memset(w2_plane_raw[:].bitcast(I32), 0)
+        nc.vector.memset(x_plane[:].bitcast(I32), 0)
+        nc.vector.memset(w_plane_raw[:].bitcast(I32), 0)
+        nc.vector.memset(wb_plane[:].bitcast(I32), 0)
+
+        ca_rows = ca.rearrange("(p t) v -> t p v", t=PACK)
+        cb_rows = cb.rearrange("(p t) v -> t p v", t=PACK)
+
+        nc.sync.dma_start(list_a[:], offs2)
+        nc.sync.dma_start(store_a[0][:], ca_rows[0])
+        nc.sync.dma_start(store_a[1][:], ca_rows[1])
+        nc.sync.dma_start(list_x[:], offs)
+        nc.sync.dma_start(x_words[:], xt_words[0].rearrange("p n t -> p (n t)").bitcast(I32))
+        nc.sync.dma_start(step_a[:], sa.rearrange("(p t) o -> p (t o)", t=PACK))
+        load_scale_rows(nc.sync, x_plane, xt_scales, 0)
+        load_scale_rows(nc.sync, x_plane, xt_scales, 1)
+        load_scale_rows(nc.sync, x_plane, xt_scales, 2)
+        nc.sync.dma_start(store_a[2][:], ca_rows[2])
+        load_scale_rows(nc.sync, x_plane, xt_scales, 3)
+        nc.sync.dma_start(store_a[3][:], ca_rows[3])
+        nc.sync.dma_start(w_raw[:].bitcast(I32), w_words[0].bitcast(I32))
+        load_scale_rows(nc.sync, w_plane_raw, w_scales, 0)
+        load_scale_rows(nc.sync, w_plane_raw, w_scales, 1)
+        load_scale_rows(nc.sync, w_plane_raw, w_scales, 2)
+        load_scale_rows(nc.sync, w_plane_raw, w_scales, 3)
+        nc.sync.dma_start(w2_raw[:], w2_words[0].rearrange("p n t -> p (n t)").bitcast(I32))
+        load_scale_rows(nc.sync, w2_plane_raw, w2_scales, 0)
+        load_scale_rows(nc.sync, w2_plane_raw, w2_scales, 1)
+        load_scale_rows(nc.sync, w2_plane_raw, w2_scales, 2)
+        load_scale_rows(nc.sync, w2_plane_raw, w2_scales, 3)
+        nc.sync.dma_start(list_b[:], offs3)
+        nc.sync.dma_start(store_b[0][:], cb_rows[0])
+        nc.sync.dma_start(step_b[:], sb.rearrange("(p t) o -> p (t o)", t=PACK))
+        nc.sync.dma_start(store_b[1][:], cb_rows[1])
+        nc.sync.dma_start(store_b[2][:], cb_rows[2])
+        nc.sync.dma_start(store_b[3][:], cb_rows[3])
+        nc.sync.dma_start(wb_codes[:], wb_words[0].rearrange("p n t -> p (n t)").bitcast(I32))
+        load_scale_rows(nc.sync, wb_plane, wb_scales, 0)
+        load_scale_rows(nc.sync, wb_plane, wb_scales, 1)
+        load_scale_rows(nc.sync, wb_plane, wb_scales, 2)
+        load_scale_rows(nc.sync, wb_plane, wb_scales, 3)
+
+        codes_a = [tile([P, J], U8, "codes_a%d" % t) for t in range(PACK)]
+        codes_b = [tile([P, J], U8, "codes_b%d" % t) for t in range(PACK)]
+        gates = [tile([P, 2 * J], F32, "gates%d" % t) for t in range(PACK)]
+        xg_words = tile([P, J], U32, "xg_words")
+        xg_plane = tile([P, J], U8, "xg_plane")
+        w_codes = tile([P, 2 * R], U8, "w_codes")
+        w2_codes = tile([P, R], U32, "w2_codes")
+        w_plane = tile([P, R], U8, "w_plane")
+        w2_plane = tile([P, R], U8, "w2_plane")
+
+        def look_up(codes, store, offsets, step, t, cols):
+            nc.vector.tensor_copy(codes[t][:], store[t][:].indirect(offsets[:]))
+            nc.scalar.activation(gates[t][:, cols], codes[t][:].bitcast(FP8), ACT.Copy, scale=step[:, t : t + 1])
+
+        def deal(engine_copy, dst, src):
+            engine_copy(dst.rearrange("p (t m) -> p t m", t=PACK), src.rearrange("p (m t) -> p t m", t=PACK))
+
+        first, second = slice(0, J), slice(J, 2 * J)
+        look_up(codes_a, store_a, list_a, step_a, 0, first)
+        look_up(codes_a, store_a, list_a, step_a, 1, first)
+        nc.vector.tensor_copy(xg_words[:], x_words[:].bitcast(U32).indirect(list_x[:]))
+        look_up(codes_a, store_a, list_a, step_a, 2, first)
+        nc.vector.tensor_copy(xg_plane[:], x_plane[:].indirect(list_x[:]))
+        look_up(codes_a, store_a, list_a, step_a, 3, first)
+        deal(nc.scalar.copy, w_codes[:].bitcast(U16), w_raw[:].bitcast(U16))
+        deal(nc.vector.tensor_copy, w_plane[:], w_plane_raw[:])
+        deal(nc.scalar.copy, w2_codes[:], w2_raw[:].bitcast(U32))
+        deal(nc.vector.tensor_copy, w2_plane[:], w2_plane_raw[:])
+
+        sums = [psum.tile([P, 2 * J], F32, name="sums%d" % t) for t in range(PACK)]
+        for t in range(PACK):
+            cols = slice(P * t, P * (t + 1))
+            nc.tensor.matmul_mx(
+                sums[t][:, first],
+                lhsT=w_codes[:, 2 * P * t : 2 * P * (t + 1)].bitcast(E2M1X4),
+                lhsT_scale=w_plane[:, cols],
+                rhs=xg_words[:].bitcast(E4M3X4),
+                rhs_scale=xg_plane[:],
+                start=True,
+                stop=True,
+            )
+            nc.tensor.matmul_mx(
+                sums[t][:, second],
+                lhsT=w2_codes[:, cols].bitcast(E5M2X4),
+                lhsT_scale=w2_plane[:, cols],
+                rhs=xg_words[:].bitcast(E4M3X4),
+                rhs_scale=xg_plane[:],
+                start=True,
+                stop=True,
+            )
+
+        for t in range(PACK):
+            look_up(codes_b, store_b, list_b, step_b, t, second)
+
+        prods = tile([P, PACK, 2, J], F32, "prods")
+        for t in range(PACK):
+            nc.vector.tensor_tensor(prods[:, t].rearrange("p s j -> p (s j)"), sums[t][:], gates[t][:], ALU.mult)
+
+        hid = [tile([P, HALF * PACK], BF16, "hid%d" % h) for h in range(2)]
+        hid_codes = [tile([P, HALF], U32, "hid_codes%d" % h) for h in range(2)]
+        hid_plane = [tile([P, HALF], U8, "hid_plane%d" % h) for h in range(2)]
+        for h in range(2):
+            js = slice(HALF * h, HALF * (h + 1))
+            nc.vector.tensor_tensor(
+                hid[h][:].rearrange("p (c i t) -> p c t i", i=RUN, t=PACK),
+                prods[:, :, 0, js].rearrange("p t (c i) -> p c t i", i=RUN),
+                prods[:, :, 1, js].rearrange("p t (c i) -> p c t i", i=RUN),
+                ALU.max,
+            )
+        for h in range(2):
+            nc.vector.quantize_mx(hid_codes[h][:].bitcast(E4M3X4), hid_plane[h][:], hid[h][:])
+
+        out_rows = out.rearrange("(g p) j -> g p j", p=P)
+        for h in range(2):
+            js = slice(HALF * h, HALF * (h + 1))
+            for g in range(N // P):
+                cols = slice(P * g, P * (g + 1))
+                acc = psum.tile([P, HALF], F32, name="acc%d_%d" % (h, g))
+                nc.tensor.matmul_mx(
+                    acc[:],
+                    lhsT=wb_codes[:, cols].bitcast(E5M2X4),
+                    lhsT_scale=wb_plane[:, cols],
+                    rhs=hid_codes[h][:].bitcast(E4M3X4),
+                    rhs_scale=hid_plane[h][:],
+                    start=True,
+                    stop=True,
+                )
+                res = tile([P, HALF], F32, "res%d_%d" % (h, g))
+                if g == 0 or h == 0:
+                    nc.scalar.copy(res[:], acc[:])
+                else:
+                    nc.vector.tensor_copy(res[:], acc[:])
+                nc.sync.dma_start(out_rows[g][:, js], res[:])

@@ -1,6 +1,7 @@
 from contextlib import ExitStack
 
 import concourse.mybir as mybir
+from concourse.masks import make_identity
 
 K, T, J, R, V, N = 512, 1024, 256, 512, 1024, 256
 FLOPS = 2 * (2 * K * R * J + R * N * J)
@@ -23,6 +24,7 @@ PACK = 4
 QUADS = 4
 HALF = J // 2
 RUN = 4
+EARLY_A = 2
 
 
 def load_scale_rows(queue, plane, scales, q):
@@ -37,8 +39,8 @@ def tile_list_twostores_kernel(
         sb_pool = ctx.enter_context(tc.tile_pool(name="keep", bufs=1))
         psum = ctx.enter_context(tc.psum_pool(name="psum", bufs=1))
 
-        def tile(shape, dtype, name):
-            return sb_pool.tile(shape, dtype, name=name, align_bytes=64)
+        def tile(shape, dtype, name, tag=None):
+            return sb_pool.tile(shape, dtype, name=name, tag=tag or name, align_bytes=64)
 
         list_x = tile([P, J // 16], U16, "list_x")
         list_a = tile([P, J // 16], U16, "list_a")
@@ -47,8 +49,8 @@ def tile_list_twostores_kernel(
         x_plane = tile([P, T], U8, "x_plane")
         w_raw = tile([P, 2 * R], U8, "w_raw")
         w2_raw = tile([P, R], I32, "w2_raw")
-        w_plane_raw = tile([P, R], U8, "w_plane_raw")
-        w2_plane_raw = tile([P, R], U8, "w2_plane_raw")
+        staged = tile([4, QUADS, 2 * R], U8, "staged")
+        spread = tile([P, 2 * R], U8, "spread")
         wb_codes = tile([P, N], I32, "wb_codes")
         wb_plane = tile([P, N], U8, "wb_plane")
         step_a = tile([P, PACK], F32, "step_a")
@@ -56,42 +58,35 @@ def tile_list_twostores_kernel(
         store_a = [tile([P, V], U8, "store_a%d" % t) for t in range(PACK)]
         store_b = [tile([P, V], U8, "store_b%d" % t) for t in range(PACK)]
 
-        nc.vector.memset(w2_plane_raw[:].bitcast(I32), 0)
         nc.vector.memset(x_plane[:].bitcast(I32), 0)
-        nc.vector.memset(w_plane_raw[:].bitcast(I32), 0)
+        nc.vector.memset(spread[:].bitcast(I32), 0)
         nc.vector.memset(wb_plane[:].bitcast(I32), 0)
 
         ca_rows = ca.rearrange("(p t) v -> t p v", t=PACK)
         cb_rows = cb.rearrange("(p t) v -> t p v", t=PACK)
 
+        nc.scalar.dma_start(staged[0:4, :, 0:R].bitcast(I32), w_scales[0].rearrange("(q r) n -> r q n", r=4).bitcast(I32))
+        nc.scalar.dma_start(staged[0:4, :, R : 2 * R].bitcast(I32), w2_scales[0].rearrange("(q r) n -> r q n", r=4).bitcast(I32))
         nc.sync.dma_start(list_a[:], offs2)
         nc.sync.dma_start(store_a[0][:], ca_rows[0])
         nc.sync.dma_start(store_a[1][:], ca_rows[1])
         nc.sync.dma_start(list_x[:], offs)
         nc.sync.dma_start(x_words[:], xt_words[0].rearrange("p n t -> p (n t)").bitcast(I32))
-        nc.sync.dma_start(step_a[:], sa.rearrange("(p t) o -> p (t o)", t=PACK))
         load_scale_rows(nc.sync, x_plane, xt_scales, 0)
         load_scale_rows(nc.sync, x_plane, xt_scales, 1)
         load_scale_rows(nc.sync, x_plane, xt_scales, 2)
-        nc.sync.dma_start(store_a[2][:], ca_rows[2])
         load_scale_rows(nc.sync, x_plane, xt_scales, 3)
-        nc.sync.dma_start(store_a[3][:], ca_rows[3])
         nc.sync.dma_start(w_raw[:].bitcast(I32), w_words[0].bitcast(I32))
-        load_scale_rows(nc.sync, w_plane_raw, w_scales, 0)
-        load_scale_rows(nc.sync, w_plane_raw, w_scales, 1)
-        load_scale_rows(nc.sync, w_plane_raw, w_scales, 2)
-        load_scale_rows(nc.sync, w_plane_raw, w_scales, 3)
+        nc.sync.dma_start(store_a[2][:], ca_rows[2])
         nc.sync.dma_start(w2_raw[:], w2_words[0].rearrange("p n t -> p (n t)").bitcast(I32))
-        load_scale_rows(nc.sync, w2_plane_raw, w2_scales, 0)
-        load_scale_rows(nc.sync, w2_plane_raw, w2_scales, 1)
-        load_scale_rows(nc.sync, w2_plane_raw, w2_scales, 2)
-        load_scale_rows(nc.sync, w2_plane_raw, w2_scales, 3)
+        nc.sync.dma_start(store_a[3][:], ca_rows[3])
         nc.sync.dma_start(list_b[:], offs3)
+        nc.sync.dma_start(step_a[:], sa.rearrange("(p t) o -> p (t o)", t=PACK))
         nc.sync.dma_start(store_b[0][:], cb_rows[0])
-        nc.sync.dma_start(step_b[:], sb.rearrange("(p t) o -> p (t o)", t=PACK))
         nc.sync.dma_start(store_b[1][:], cb_rows[1])
         nc.sync.dma_start(store_b[2][:], cb_rows[2])
         nc.sync.dma_start(store_b[3][:], cb_rows[3])
+        nc.sync.dma_start(step_b[:], sb.rearrange("(p t) o -> p (t o)", t=PACK))
         nc.sync.dma_start(wb_codes[:], wb_words[0].rearrange("p n t -> p (n t)").bitcast(I32))
         load_scale_rows(nc.sync, wb_plane, wb_scales, 0)
         load_scale_rows(nc.sync, wb_plane, wb_scales, 1)
@@ -100,61 +95,66 @@ def tile_list_twostores_kernel(
 
         codes_a = [tile([P, J], U8, "codes_a%d" % t) for t in range(PACK)]
         codes_b = [tile([P, J], U8, "codes_b%d" % t) for t in range(PACK)]
-        gates = [tile([P, 2 * J], F32, "gates%d" % t) for t in range(PACK)]
+        gates = [[tile([P, 2 * J], F32, "gates%d_%d" % (s, u)) for u in range(2)] for s in range(2)]
         xg_words = tile([P, J], U32, "xg_words")
         xg_plane = tile([P, J], U8, "xg_plane")
-        w_codes = tile([P, 2 * R], U8, "w_codes")
-        w2_codes = tile([P, R], U32, "w2_codes")
-        w_plane = tile([P, R], U8, "w_plane")
-        w2_plane = tile([P, R], U8, "w2_plane")
+        identity = tile([P, P], F32, "identity")
+        make_identity(nc, identity[:])
 
-        def look_up(codes, store, offsets, step, t, cols):
+        def look_up(s, t):
+            codes, store, offsets, step = ((codes_a, store_a, list_a, step_a), (codes_b, store_b, list_b, step_b))[s]
             nc.vector.tensor_copy(codes[t][:], store[t][:].indirect(offsets[:]))
-            nc.scalar.activation(gates[t][:, cols], codes[t][:].bitcast(FP8), ACT.Copy, scale=step[:, t : t + 1])
+            nc.scalar.activation(
+                gates[s][t // 2][:, J * (t % 2) : J * (t % 2 + 1)], codes[t][:].bitcast(FP8), ACT.Copy, scale=step[:, t : t + 1]
+            )
 
-        def deal(engine_copy, dst, src):
-            engine_copy(dst.rearrange("p (t m) -> p t m", t=PACK), src.rearrange("p (m t) -> p t m", t=PACK))
-
-        first, second = slice(0, J), slice(J, 2 * J)
-        look_up(codes_a, store_a, list_a, step_a, 0, first)
-        look_up(codes_a, store_a, list_a, step_a, 1, first)
+        nc.scalar.copy(spread[0:4, :].bitcast(U32), staged[0:4, 0, :].bitcast(U32))
+        for q in range(1, QUADS):
+            nc.vector.tensor_copy(spread[32 * q : 32 * q + 4, :].bitcast(I32), staged[0:4, q, :].bitcast(I32))
+        for t in range(EARLY_A):
+            look_up(0, t)
         nc.vector.tensor_copy(xg_words[:], x_words[:].bitcast(U32).indirect(list_x[:]))
-        look_up(codes_a, store_a, list_a, step_a, 2, first)
         nc.vector.tensor_copy(xg_plane[:], x_plane[:].indirect(list_x[:]))
-        look_up(codes_a, store_a, list_a, step_a, 3, first)
-        deal(nc.scalar.copy, w_codes[:].bitcast(U16), w_raw[:].bitcast(U16))
-        deal(nc.vector.tensor_copy, w_plane[:], w_plane_raw[:])
-        deal(nc.scalar.copy, w2_codes[:], w2_raw[:].bitcast(U32))
-        deal(nc.vector.tensor_copy, w2_plane[:], w2_plane_raw[:])
 
-        sums = [psum.tile([P, 2 * J], F32, name="sums%d" % t) for t in range(PACK)]
-        for t in range(PACK):
-            cols = slice(P * t, P * (t + 1))
-            nc.tensor.matmul_mx(
-                sums[t][:, first],
-                lhsT=w_codes[:, 2 * P * t : 2 * P * (t + 1)].bitcast(E2M1X4),
-                lhsT_scale=w_plane[:, cols],
-                rhs=xg_words[:].bitcast(E4M3X4),
-                rhs_scale=xg_plane[:],
-                start=True,
-                stop=True,
-            )
-            nc.tensor.matmul_mx(
-                sums[t][:, second],
-                lhsT=w2_codes[:, cols].bitcast(E5M2X4),
-                lhsT_scale=w2_plane[:, cols],
-                rhs=xg_words[:].bitcast(E4M3X4),
-                rhs_scale=xg_plane[:],
-                start=True,
-                stop=True,
-            )
+        weights = (w_raw[:].bitcast(E2M1X4), w2_raw[:].bitcast(E5M2X4))
+        sums = [[psum.tile([P, 2 * J], F32, name="sums%d_%d" % (s, u)) for u in range(2)] for s in range(2)]
+        rows = [[tile([P, PACK, P], F32, "rows%d_%d" % (s, h)) for h in range(2)] for s in range(2)]
+        for s in range(2):
+            for h in range(2):
+                js = slice(HALF * h, HALF * (h + 1))
+                by_slot = psum.tile([P, R], F32, name="by_slot%d_%d" % (s, h), tag="bank%d_%d" % (s, h))
+                nc.tensor.matmul_mx(
+                    by_slot[:],
+                    lhsT=xg_words[:, js].bitcast(E4M3X4),
+                    lhsT_scale=xg_plane[:, js],
+                    rhs=weights[s],
+                    rhs_scale=spread[:, R * s : R * (s + 1)],
+                    start=True,
+                    stop=True,
+                )
+                nc.scalar.copy(rows[s][h][:], by_slot[:].rearrange("p (m t) -> p t m", t=PACK))
+        for s in range(2):
+            for h in range(2):
+                for t in range(PACK):
+                    col = J * (t % 2) + HALF * h
+                    nc.tensor.transpose(sums[s][t // 2][:, col : col + HALF], rows[s][h][:, t, :], identity[:])
 
+        for t in range(EARLY_A, PACK):
+            look_up(0, t)
         for t in range(PACK):
-            look_up(codes_b, store_b, list_b, step_b, t, second)
+            look_up(1, t)
 
-        prods = tile([P, PACK, 2, J], F32, "prods")
-        for t in range(PACK):
-            nc.vector.tensor_tensor(prods[:, t].rearrange("p s j -> p (s j)"), sums[t][:], gates[t][:], ALU.mult)
+        prods = [tile([P, PACK, J], F32, "prods0", tag="store_b3"), tile([P, PACK, J], F32, "prods1")]
+        for s in range(2):
+            for u in range(2):
+                pieces = [slice(0, HALF), slice(HALF, J)] if (s, u) == (1, 1) else [slice(0, J)]
+                for js in pieces:
+                    nc.vector.tensor_tensor(
+                        prods[s][:, 2 * u : 2 * u + 2, js],
+                        sums[s][u][:].rearrange("p (t j) -> p t j", t=2)[:, :, js],
+                        gates[s][u][:].rearrange("p (t j) -> p t j", t=2)[:, :, js],
+                        ALU.mult,
+                    )
 
         hid = [tile([P, HALF * PACK], BF16, "hid%d" % h) for h in range(2)]
         hid_codes = [tile([P, HALF], U32, "hid_codes%d" % h) for h in range(2)]
@@ -163,8 +163,8 @@ def tile_list_twostores_kernel(
             js = slice(HALF * h, HALF * (h + 1))
             nc.vector.tensor_tensor(
                 hid[h][:].rearrange("p (c i t) -> p c t i", i=RUN, t=PACK),
-                prods[:, :, 0, js].rearrange("p t (c i) -> p c t i", i=RUN),
-                prods[:, :, 1, js].rearrange("p t (c i) -> p c t i", i=RUN),
+                prods[0][:, :, js].rearrange("p t (c i) -> p c t i", i=RUN),
+                prods[1][:, :, js].rearrange("p t (c i) -> p c t i", i=RUN),
                 ALU.max,
             )
         for h in range(2):
@@ -175,7 +175,7 @@ def tile_list_twostores_kernel(
             js = slice(HALF * h, HALF * (h + 1))
             for g in range(N // P):
                 cols = slice(P * g, P * (g + 1))
-                acc = psum.tile([P, HALF], F32, name="acc%d_%d" % (h, g))
+                acc = psum.tile([P, HALF], F32, name="acc%d_%d" % (h, g), tag="bank%d_%d" % (h, g))
                 nc.tensor.matmul_mx(
                     acc[:],
                     lhsT=wb_codes[:, cols].bitcast(E5M2X4),
@@ -186,8 +186,9 @@ def tile_list_twostores_kernel(
                     stop=True,
                 )
                 res = tile([P, HALF], F32, "res%d_%d" % (h, g))
-                if g == 0 or h == 0:
-                    nc.scalar.copy(res[:], acc[:])
-                else:
+                if (h, g) == (1, 1):
                     nc.vector.tensor_copy(res[:], acc[:])
-                nc.sync.dma_start(out_rows[g][:, js], res[:])
+                else:
+                    nc.scalar.copy(res[:], acc[:])
+                queue = nc.scalar if (h, g) == (1, 0) else nc.sync
+                queue.dma_start(out_rows[g][:, js], res[:])

@@ -23,7 +23,7 @@ P = 128
 PACK = 4
 QUADS = 4
 HALF = J // 2
-RUN = 4
+RUN = 2
 EARLY_A = 2
 
 

from contextlib import ExitStack

import concourse.mybir as mybir
from concourse.masks import make_identity

K, T, J, R, V, N = 512, 1024, 256, 512, 1024, 256
FLOPS = 2 * (2 * K * R * J + R * N * J)

F32 = mybir.dt.float32
BF16 = mybir.dt.bfloat16
I32 = mybir.dt.int32
U32 = mybir.dt.uint32
U16 = mybir.dt.uint16
U8 = mybir.dt.uint8
FP8 = mybir.dt.float8_e4m3fn
E4M3X4 = mybir.dt.float8_e4m3fn_x4
E5M2X4 = mybir.dt.float8_e5m2_x4
E2M1X4 = mybir.dt.float4_e2m1fn_x4
ALU = mybir.AluOpType
ACT = mybir.ActivationFunctionType

P = 128
PACK = 4
QUADS = 4
HALF = J // 2
RUN = 2
EARLY_A = 2


def load_scale_rows(queue, plane, scales, q):
    queue.dma_start(plane[32 * q : 32 * q + 4, :].bitcast(I32), scales[0, 4 * q : 4 * q + 4, :].bitcast(I32))


def tile_list_twostores_kernel(
    tc, xt_words, xt_scales, w_words, w_scales, w2_words, w2_scales, ca, cb, sa, sb, wb_words, wb_scales, offs, offs2, offs3, out
):
    nc = tc.nc
    with ExitStack() as ctx:
        sb_pool = ctx.enter_context(tc.tile_pool(name="keep", bufs=1))
        psum = ctx.enter_context(tc.psum_pool(name="psum", bufs=1))

        def tile(shape, dtype, name, tag=None):
            return sb_pool.tile(shape, dtype, name=name, tag=tag or name, align_bytes=64)

        list_x = tile([P, J // 16], U16, "list_x")
        list_a = tile([P, J // 16], U16, "list_a")
        list_b = tile([P, J // 16], U16, "list_b")
        x_words = tile([P, T], I32, "x_words")
        x_plane = tile([P, T], U8, "x_plane")
        w_raw = tile([P, 2 * R], U8, "w_raw")
        w2_raw = tile([P, R], I32, "w2_raw")
        staged = tile([4, QUADS, 2 * R], U8, "staged")
        spread = tile([P, 2 * R], U8, "spread")
        wb_codes = tile([P, N], I32, "wb_codes")
        wb_plane = tile([P, N], U8, "wb_plane")
        step_a = tile([P, PACK], F32, "step_a")
        step_b = tile([P, PACK], F32, "step_b")
        store_a = [tile([P, V], U8, "store_a%d" % t) for t in range(PACK)]
        store_b = [tile([P, V], U8, "store_b%d" % t) for t in range(PACK)]

        nc.vector.memset(x_plane[:].bitcast(I32), 0)
        nc.vector.memset(spread[:].bitcast(I32), 0)
        nc.vector.memset(wb_plane[:].bitcast(I32), 0)

        ca_rows = ca.rearrange("(p t) v -> t p v", t=PACK)
        cb_rows = cb.rearrange("(p t) v -> t p v", t=PACK)

        nc.scalar.dma_start(staged[0:4, :, 0:R].bitcast(I32), w_scales[0].rearrange("(q r) n -> r q n", r=4).bitcast(I32))
        nc.scalar.dma_start(staged[0:4, :, R : 2 * R].bitcast(I32), w2_scales[0].rearrange("(q r) n -> r q n", r=4).bitcast(I32))
        nc.sync.dma_start(list_a[:], offs2)
        nc.sync.dma_start(store_a[0][:], ca_rows[0])
        nc.sync.dma_start(store_a[1][:], ca_rows[1])
        nc.sync.dma_start(list_x[:], offs)
        nc.sync.dma_start(x_words[:], xt_words[0].rearrange("p n t -> p (n t)").bitcast(I32))
        load_scale_rows(nc.sync, x_plane, xt_scales, 0)
        load_scale_rows(nc.sync, x_plane, xt_scales, 1)
        load_scale_rows(nc.sync, x_plane, xt_scales, 2)
        load_scale_rows(nc.sync, x_plane, xt_scales, 3)
        nc.sync.dma_start(w_raw[:].bitcast(I32), w_words[0].bitcast(I32))
        nc.sync.dma_start(store_a[2][:], ca_rows[2])
        nc.sync.dma_start(w2_raw[:], w2_words[0].rearrange("p n t -> p (n t)").bitcast(I32))
        nc.sync.dma_start(store_a[3][:], ca_rows[3])
        nc.sync.dma_start(list_b[:], offs3)
        nc.sync.dma_start(step_a[:], sa.rearrange("(p t) o -> p (t o)", t=PACK))
        nc.sync.dma_start(store_b[0][:], cb_rows[0])
        nc.sync.dma_start(store_b[1][:], cb_rows[1])
        nc.sync.dma_start(store_b[2][:], cb_rows[2])
        nc.sync.dma_start(store_b[3][:], cb_rows[3])
        nc.sync.dma_start(step_b[:], sb.rearrange("(p t) o -> p (t o)", t=PACK))
        nc.sync.dma_start(wb_codes[:], wb_words[0].rearrange("p n t -> p (n t)").bitcast(I32))
        load_scale_rows(nc.sync, wb_plane, wb_scales, 0)
        load_scale_rows(nc.sync, wb_plane, wb_scales, 1)
        load_scale_rows(nc.sync, wb_plane, wb_scales, 2)
        load_scale_rows(nc.sync, wb_plane, wb_scales, 3)

        codes_a = [tile([P, J], U8, "codes_a%d" % t) for t in range(PACK)]
        codes_b = [tile([P, J], U8, "codes_b%d" % t) for t in range(PACK)]
        gates = [[tile([P, 2 * J], F32, "gates%d_%d" % (s, u)) for u in range(2)] for s in range(2)]
        xg_words = tile([P, J], U32, "xg_words")
        xg_plane = tile([P, J], U8, "xg_plane")
        identity = tile([P, P], F32, "identity")
        make_identity(nc, identity[:])

        def look_up(s, t):
            codes, store, offsets, step = ((codes_a, store_a, list_a, step_a), (codes_b, store_b, list_b, step_b))[s]
            nc.vector.tensor_copy(codes[t][:], store[t][:].indirect(offsets[:]))
            nc.scalar.activation(
                gates[s][t // 2][:, J * (t % 2) : J * (t % 2 + 1)], codes[t][:].bitcast(FP8), ACT.Copy, scale=step[:, t : t + 1]
            )

        nc.scalar.copy(spread[0:4, :].bitcast(U32), staged[0:4, 0, :].bitcast(U32))
        for q in range(1, QUADS):
            nc.vector.tensor_copy(spread[32 * q : 32 * q + 4, :].bitcast(I32), staged[0:4, q, :].bitcast(I32))
        for t in range(EARLY_A):
            look_up(0, t)
        nc.vector.tensor_copy(xg_words[:], x_words[:].bitcast(U32).indirect(list_x[:]))
        nc.vector.tensor_copy(xg_plane[:], x_plane[:].indirect(list_x[:]))

        weights = (w_raw[:].bitcast(E2M1X4), w2_raw[:].bitcast(E5M2X4))
        sums = [[psum.tile([P, 2 * J], F32, name="sums%d_%d" % (s, u)) for u in range(2)] for s in range(2)]
        rows = [[tile([P, PACK, P], F32, "rows%d_%d" % (s, h)) for h in range(2)] for s in range(2)]
        for s in range(2):
            for h in range(2):
                js = slice(HALF * h, HALF * (h + 1))
                by_slot = psum.tile([P, R], F32, name="by_slot%d_%d" % (s, h), tag="bank%d_%d" % (s, h))
                nc.tensor.matmul_mx(
                    by_slot[:],
                    lhsT=xg_words[:, js].bitcast(E4M3X4),
                    lhsT_scale=xg_plane[:, js],
                    rhs=weights[s],
                    rhs_scale=spread[:, R * s : R * (s + 1)],
                    start=True,
                    stop=True,
                )
                nc.scalar.copy(rows[s][h][:], by_slot[:].rearrange("p (m t) -> p t m", t=PACK))
        for s in range(2):
            for h in range(2):
                for t in range(PACK):
                    col = J * (t % 2) + HALF * h
                    nc.tensor.transpose(sums[s][t // 2][:, col : col + HALF], rows[s][h][:, t, :], identity[:])

        for t in range(EARLY_A, PACK):
            look_up(0, t)
        for t in range(PACK):
            look_up(1, t)

        prods = [tile([P, PACK, J], F32, "prods0", tag="store_b3"), tile([P, PACK, J], F32, "prods1")]
        for s in range(2):
            for u in range(2):
                pieces = [slice(0, HALF), slice(HALF, J)] if (s, u) == (1, 1) else [slice(0, J)]
                for js in pieces:
                    nc.vector.tensor_tensor(
                        prods[s][:, 2 * u : 2 * u + 2, js],
                        sums[s][u][:].rearrange("p (t j) -> p t j", t=2)[:, :, js],
                        gates[s][u][:].rearrange("p (t j) -> p t j", t=2)[:, :, js],
                        ALU.mult,
                    )

        hid = [tile([P, HALF * PACK], BF16, "hid%d" % h) for h in range(2)]
        hid_codes = [tile([P, HALF], U32, "hid_codes%d" % h) for h in range(2)]
        hid_plane = [tile([P, HALF], U8, "hid_plane%d" % h) for h in range(2)]
        for h in range(2):
            js = slice(HALF * h, HALF * (h + 1))
            nc.vector.tensor_tensor(
                hid[h][:].rearrange("p (c i t) -> p c t i", i=RUN, t=PACK),
                prods[0][:, :, js].rearrange("p t (c i) -> p c t i", i=RUN),
                prods[1][:, :, js].rearrange("p t (c i) -> p c t i", i=RUN),
                ALU.max,
            )
        for h in range(2):
            nc.vector.quantize_mx(hid_codes[h][:].bitcast(E4M3X4), hid_plane[h][:], hid[h][:])

        out_rows = out.rearrange("(g p) j -> g p j", p=P)
        for h in range(2):
            js = slice(HALF * h, HALF * (h + 1))
            for g in range(N // P):
                cols = slice(P * g, P * (g + 1))
                acc = psum.tile([P, HALF], F32, name="acc%d_%d" % (h, g), tag="bank%d_%d" % (h, g))
                nc.tensor.matmul_mx(
                    acc[:],
                    lhsT=wb_codes[:, cols].bitcast(E5M2X4),
                    lhsT_scale=wb_plane[:, cols],
                    rhs=hid_codes[h][:].bitcast(E4M3X4),
                    rhs_scale=hid_plane[h][:],
                    start=True,
                    stop=True,
                )
                res = tile([P, HALF], F32, "res%d_%d" % (h, g))
                if (h, g) == (1, 1):
                    nc.vector.tensor_copy(res[:], acc[:])
                else:
                    nc.scalar.copy(res[:], acc[:])
                queue = nc.scalar if (h, g) == (1, 0) else nc.sync
                queue.dma_start(out_rows[g][:, js], res[:])
